import numpy as np
import ml_dtypes


def mxq(x, axis, fmt="e4m3"):
    dtype, down = {"e4m3": (ml_dtypes.float8_e4m3fn, 7), "e5m2": (ml_dtypes.float8_e5m2, 14)}[fmt]
    v = np.moveaxis(np.asarray(x, np.float32).astype(ml_dtypes.bfloat16).astype(np.float64), axis, -1)
    blocks = v.reshape(v.shape[:-1] + (-1, 32))
    amax = np.abs(blocks).max(-1, keepdims=True)
    byte = np.maximum(np.where(amax > 0, np.frexp(amax)[1] - 1 + 127, 0) - down, 1)
    scale = np.exp2(byte - 127.0)
    codes = (blocks / scale).astype(np.float32).astype(dtype).astype(np.float64)
    return np.moveaxis((codes * scale).reshape(v.shape), -1, axis)


WIDE = False


def mx_kscale(k):
    if not WIDE:
        return np.ones(k)
    levels = np.array([30, -30])
    if k % 512:
        return np.exp2(np.random.permutation(np.resize(levels, k // 32))).repeat(32)
    a = np.empty((k // 512, 16))
    for p in range(k // 512):
        a[p, :8] = np.random.permutation(np.resize(levels, 8))
        for g in range(8):
            far = levels[np.abs(levels - a[p, g]) >= 10]
            a[p, g + 8] = far[np.random.randint(len(far))]
    return np.exp2(a.ravel()).repeat(32)


def f64(x):
    return np.asarray(x).astype(np.float64)


def striped(idx):
    return np.tile(np.asarray(idx).reshape(-1, 16).T, (8, 1)).astype(np.uint16)


def unstriped(offs):
    return offs[:16].T.reshape(-1).astype(np.int64)


E2M1 = np.array([0.0, 0.5, 1.0, 1.5, 2.0, 3.0, 4.0, 6.0, -0.0, -0.5, -1.0, -1.5, -2.0, -3.0, -4.0, -6.0])


def pack_weight(w, fmt):
    k, n = w.shape
    w = f64(np.asarray(w, np.float32).astype(ml_dtypes.bfloat16)).reshape(k // 32, 32, n)
    amax = np.abs(w).max(1)
    if fmt == "e4m3":
        byte = np.frexp(amax)[1] - 1 + 127 - 7
    else:
        mant, ex = np.frexp(amax / 6.0)
        byte = np.where(mant > 0.5, ex, ex - 1) + 127
    byte = np.clip(np.where(amax > 0, byte, 1), 1, 254)
    scaled = (w * np.exp2(127.0 - byte)[:, None, :]).reshape(k, n).astype(np.float32)
    by_word = np.ascontiguousarray(scaled.reshape(k // 512, 128, 4, n).transpose(0, 1, 3, 2))
    if fmt == "e4m3":
        words = by_word.astype(ml_dtypes.float8_e4m3fn).view(np.uint8)
    else:
        c = by_word.astype(ml_dtypes.float4_e2m1fn).view(np.uint8) & 0xF
        words = (c[..., 0::2] | (c[..., 1::2] << 4)).reshape(k // 512, 128, 2 * n)
    return np.ascontiguousarray(words), np.ascontiguousarray(byte.astype(np.uint8).reshape(k // 512, 16, n))


def unpack_weight(words, scales, fmt):
    g, _, n = scales.shape
    words = np.ascontiguousarray(words).reshape(g, 128, n, -1)
    if fmt == "e4m3":
        vals = words.view(ml_dtypes.float8_e4m3fn).astype(np.float64)
    else:
        nib = np.empty((g, 128, n, 4), np.uint8)
        nib[..., 0::2] = words & 0xF
        nib[..., 1::2] = words >> 4
        vals = E2M1[nib]
    vals = vals * np.repeat(np.exp2(scales.astype(np.float64) - 127.0), 8, axis=1)[..., None]
    return vals.transpose(0, 1, 3, 2).reshape(g * 512, n)


def bf(x):
    return np.asarray(x, np.float32).astype(ml_dtypes.bfloat16)


def planes(Y):
    r, m = Y.shape
    b = f64(bf(Y)).reshape(r // 32, 32, m)
    amax = np.abs(b).max(1)
    byte = np.clip(np.where(amax > 0, np.frexp(amax)[1] - 1 + 127 - 7, 1), 1, 254)
    codes = (b * np.exp2(127.0 - byte)[:, None, :]).reshape(r, m).astype(np.float32).astype(ml_dtypes.float8_e4m3fn).view(np.uint8)
    words = codes.reshape(r // 512, 128, 4, m).transpose(0, 1, 3, 2)
    return np.ascontiguousarray(words), np.ascontiguousarray(byte.astype(np.uint8).reshape(r // 512, 16, m))


K, R, N, T, J = 512, 512, 512, 1024, 512


def setup_inputs():
    n = np.random.standard_normal
    idx = np.random.permutation(T)[:J]
    fn = mx_kscale(N)
    fr = mx_kscale(R)
    wdp = pack_weight(n((N, R)) * 1 / np.sqrt(N) * fn[:, None], "e4m3")
    wap = pack_weight(n((R, K)) * 1 / np.sqrt(R) / fr[:, None], "e2m1")
    wup = pack_weight(n((R, K)) * 1 / np.sqrt(R) / fr[:, None], "e4m3")
    return {
        "g": (n((N, T)) * np.exp(0.5 * n((1, T))) / fn[:, None]).astype(np.float32),
        "wd_words": wdp[0],
        "wd_scales": wdp[1],
        "va": (n((R, T)) * fr[:, None]).astype(np.float32),
        "u": (n((R, T)) * fr[:, None]).astype(np.float32),
        "wa_words": wap[0],
        "wa_scales": wap[1],
        "wu_words": wup[0],
        "wu_scales": wup[1],
        "offs": striped(idx),
    }


def reference(g, wd_words, wd_scales, va, u, wa_words, wa_scales, wu_words, wu_scales, offs):
    idx = unstriped(offs)
    wdu = unpack_weight(wd_words, wd_scales, "e4m3")
    wau = unpack_weight(wa_words, wa_scales, "e2m1")
    wuu = unpack_weight(wu_words, wu_scales, "e4m3")
    gidxq = mxq(f64(g)[:, idx], 0, "e5m2")
    dh = wdu.T @ gidxq
    da = dh * f64(u)[:, idx]
    du = dh * f64(va)[:, idx]
    daq = mxq(da, 0, "e5m2")
    duq = mxq(du, 0, "e4m3")
    y = wau.T @ daq + wuu.T @ duq
    words, scales = planes(y)
    return y, words, scales

@@ -1,0 +1,213 @@
+from contextlib import ExitStack
+
+import concourse.mybir as mybir
+
+K, R, N, T, J = 512, 512, 512, 1024, 512
+FLOPS = 3 * 2 * 512 * 512 * J
+
+F32 = mybir.dt.float32
+BF16 = mybir.dt.bfloat16
+I32 = mybir.dt.int32
+U16 = mybir.dt.uint16
+U8 = mybir.dt.uint8
+E4M3 = mybir.dt.float8_e4m3fn_x4
+E5M2 = mybir.dt.float8_e5m2_x4
+E2M1 = mybir.dt.float4_e2m1fn_x4
+MULT = mybir.AluOpType.mult
+
+P = 128
+PACK = 4
+H = J // 2
+
+
+def weave(copy, grouped, planes, lo, hi):
+    copy(
+        out=grouped[:, PACK * lo : PACK * hi].rearrange("p (c i t) -> p c t i", i=4, t=PACK),
+        in_=planes[:, :, lo:hi].rearrange("p t (c i) -> p c t i", i=4),
+    )
+
+
+def tile_list_product_unit_back_pl_kernel(
+    tc, g, wd_words, wd_scales, va, u, wa_words, wa_scales, wu_words, wu_scales, offs, out_0, out_1, out_2
+):
+    nc = tc.nc
+    with ExitStack() as ctx:
+        sb = ctx.enter_context(tc.tile_pool(name="sb", bufs=1))
+        ps = ctx.enter_context(tc.psum_pool(name="ps", bufs=1))
+
+        offsets = sb.tile([P, J // 16], U16, name="offsets")
+        g_pl = [sb.tile([P, T], F32, name="g%d" % t) for t in range(PACK)]
+        u_pl = [sb.tile([P, T], F32, name="u%d" % t) for t in range(PACK)]
+        va_pl = [sb.tile([P, T], F32, name="va%d" % t) for t in range(PACK)]
+        wd_raw = sb.tile([P, R], I32, name="wd_raw")
+        wu_raw = sb.tile([P, K], I32, name="wu_raw")
+        wa_raw = sb.tile([P, 2 * K], U8, name="wa_raw")
+        sd_raw = sb.tile([P, R], U8, name="sd_raw")
+        sau_raw = sb.tile([P, K], U8, name="sau_raw")
+
+        nc.gpsimd.memset(sd_raw[:].bitcast(I32), 0)
+        nc.gpsimd.memset(sau_raw[:].bitcast(I32), 0)
+
+        def load_plane(tile, src, t):
+            nc.sync.dma_start(out=tile[:], in_=src.rearrange("(p t) c -> p t c", t=PACK)[:, t, :])
+
+        def load_scales(tile, src, first, q):
+            nc.sync.dma_start(
+                out=tile[32 * q + first : 32 * q + first + 4, :].bitcast(I32),
+                in_=src[0, 4 * q : 4 * q + 4, :].bitcast(I32),
+            )
+
+        nc.sync.dma_start(offsets[:], offs)
+        load_plane(g_pl[0], g, 0)
+        for q in range(4):
+            load_scales(sd_raw, wd_scales, 0, q)
+        for t in range(1, PACK):
+            load_plane(g_pl[t], g, t)
+        nc.sync.dma_start(out=wd_raw[:], in_=wd_words[0].rearrange("p c t -> p (c t)").bitcast(I32))
+        for q in range(4):
+            load_scales(sau_raw, wa_scales, 0, q)
+        nc.sync.dma_start(out=wu_raw[:], in_=wu_words[0].rearrange("p c t -> p (c t)").bitcast(I32))
+        nc.sync.dma_start(out=wa_raw[:].bitcast(I32), in_=wa_words[0].bitcast(I32))
+        load_plane(u_pl[0], u, 0)
+        for q in range(4):
+            load_scales(sau_raw, wu_scales, 4, q)
+        for t in range(1, PACK):
+            load_plane(u_pl[t], u, t)
+        for t in range(PACK):
+            load_plane(va_pl[t], va, t)
+
+        def deal_words(dealt, raw):
+            nc.vector.tensor_copy(
+                out=dealt[:].rearrange("p (t c i) -> p c t i", t=PACK, i=4),
+                in_=raw[:].rearrange("p (c i t) -> p c t i", t=PACK, i=4),
+            )
+
+        def deal_scales(dealt, raw):
+            nc.vector.tensor_copy(
+                out=dealt[:].rearrange("p (t m) -> p t m", t=PACK),
+                in_=raw[:].rearrange("p (m t) -> p t m", t=PACK),
+            )
+
+        g_pick = sb.tile([P, PACK, J], F32, name="g_pick")
+        for t in range(PACK - 1):
+            nc.vector.tensor_copy(g_pick[:, t, :], g_pl[t][:].indirect(offsets[:]))
+        for h in range(2):
+            nc.vector.tensor_copy(
+                g_pick[:, PACK - 1, h * H : (h + 1) * H],
+                g_pl[PACK - 1][:].indirect(offsets[:, h * H // 16 : (h + 1) * H // 16]),
+            )
+        wd_w = sb.tile([P, R], I32, name="wd_w", align_bytes=64)
+        wd_s = sb.tile([P, R], U8, name="wd_s", align_bytes=64)
+        deal_scales(wd_s, sd_raw)
+        deal_words(wd_w, wd_raw)
+        g_bf = sb.tile([P, PACK * J], BF16, name="g_bf", tag="after_g", align_bytes=64)
+        weave(nc.scalar.copy, g_bf, g_pick, 0, H)
+        weave(nc.vector.tensor_copy, g_bf, g_pick, H, J)
+        g_w = sb.tile([P, J], I32, name="g_w", align_bytes=64)
+        g_s = sb.tile([P, J], U8, name="g_s", align_bytes=64)
+        nc.vector.quantize_mx(out=g_w[:].bitcast(E5M2), scales=g_s[:], in_=g_bf[:])
+
+        dh = [sb.tile([P, J], F32, name="dh%d" % t) for t in range(PACK - 1)]
+        dh_last = [
+            sb.tile([P, H], F32, name="dh_last0", tag="turn", align_bytes=64),
+            sb.tile([P, H], F32, name="dh_last1"),
+        ]
+        for t in range(PACK):
+            cols = slice(t * P, (t + 1) * P)
+            acc = ps.tile([P, J], F32, name="dh_acc%d" % t)
+            nc.tensor.matmul_mx(
+                out=acc[:], lhsT=wd_w[:, cols].bitcast(E4M3), lhsT_scale=wd_s[:, cols],
+                rhs=g_w[:].bitcast(E5M2), rhs_scale=g_s[:], start=True, stop=True,
+            )
+            if t < PACK - 1:
+                nc.scalar.copy(out=dh[t][:], in_=acc[:])
+            else:
+                for h in range(2):
+                    nc.scalar.copy(out=dh_last[h][:], in_=acc[:, h * H : (h + 1) * H])
+
+        def dh_half(t, h):
+            return dh[t][:, h * H : (h + 1) * H] if t < PACK - 1 else dh_last[h][:]
+
+        def half_list(h):
+            return offsets[:, h * H // 16 : (h + 1) * H // 16]
+
+        second = sb.tile([P, 7 * K], U8, name="second", tag="after_g", align_bytes=64)
+        wu_w = second[:, 0 : 4 * K].bitcast(I32)
+        wa_w = second[:, 4 * K : 6 * K]
+        wau_s = second[:, 6 * K : 7 * K]
+        deal_words(wu_w, wu_raw)
+        nc.vector.tensor_copy(
+            out=wa_w[:].rearrange("p (t m b) -> p t m b", t=PACK, b=2),
+            in_=wa_raw[:].rearrange("p (m t b) -> p t m b", t=PACK, b=2),
+        )
+        deal_scales(wau_s, sau_raw)
+
+        da = sb.tile([P, PACK, J], F32, name="da")
+        for t in range(PACK - 1):
+            nc.vector.tensor_tensor(da[:, t, :], u_pl[t][:].indirect(offsets[:]), dh[t][:], MULT)
+        for h in range(2):
+            nc.vector.tensor_tensor(
+                da[:, PACK - 1, h * H : (h + 1) * H], u_pl[PACK - 1][:].indirect(half_list(h)), dh_last[h][:], MULT
+            )
+        da_bf = sb.tile([P, PACK * J], BF16, name="da_bf", tag="after_da", align_bytes=64)
+        weave(nc.scalar.copy, da_bf, da, 0, J)
+
+        du0 = sb.tile([P, PACK, H], F32, name="du0")
+        for t in range(PACK):
+            nc.vector.tensor_tensor(du0[:, t, :], va_pl[t][:].indirect(half_list(0)), dh_half(t, 0), MULT)
+        da_w = sb.tile([P, J], I32, name="da_w", tag="turn", align_bytes=64)
+        da_s = sb.tile([P, J], U8, name="da_s", align_bytes=64)
+        nc.vector.quantize_mx(out=da_w[:].bitcast(E5M2), scales=da_s[:], in_=da_bf[:])
+        du0_bf = sb.tile([P, PACK * H], BF16, name="du0_bf", align_bytes=64)
+        weave(nc.scalar.copy, du0_bf, du0, 0, H)
+
+        y_acc = [ps.tile([P, J], F32, name="y_acc%d" % t) for t in range(PACK)]
+        for t in range(PACK):
+            cols = slice(t * P, (t + 1) * P)
+            nc.tensor.matmul_mx(
+                out=y_acc[t][:], lhsT=wa_w[:, 2 * t * P : 2 * (t + 1) * P].bitcast(E2M1), lhsT_scale=wau_s[:, cols],
+                rhs=da_w[:].bitcast(E5M2), rhs_scale=da_s[:], start=True, stop=False,
+            )
+
+        du1 = sb.tile([P, PACK, H], F32, name="du1", tag="after_da", align_bytes=64)
+        for t in range(PACK):
+            nc.vector.tensor_tensor(du1[:, t, :], va_pl[t][:].indirect(half_list(1)), dh_half(t, 1), MULT)
+        du1_bf = sb.tile([P, PACK * H], BF16, name="du1_bf", align_bytes=64)
+        weave(nc.scalar.copy, du1_bf, du1, 0, 96)
+        weave(nc.vector.tensor_copy, du1_bf, du1, 96, H)
+
+        for h, src in enumerate((du0_bf, du1_bf)):
+            du_w = sb.tile([P, H], I32, name="du_w%d" % h, align_bytes=64)
+            du_s = sb.tile([P, H], U8, name="du_s%d" % h, align_bytes=64)
+            nc.vector.quantize_mx(out=du_w[:].bitcast(E4M3), scales=du_s[:], in_=src[:])
+            for t in range(PACK):
+                cols = slice(t * P, (t + 1) * P)
+                nc.tensor.matmul_mx(
+                    out=y_acc[t][:, h * H : (h + 1) * H], lhsT=wu_w[:, cols].bitcast(E4M3),
+                    lhsT_scale=wau_s[4:P, cols],
+                    rhs=du_w[:].bitcast(E4M3), rhs_scale=du_s[:], start=False, stop=(h == 1),
+                )
+
+        y = sb.tile([P, PACK, J], F32, name="y")
+        y_rows = out_0.rearrange("(p t) j -> p t j", t=PACK)
+        for pair in range(2):
+            nc.scalar.copy(out=y[:, 2 * pair, :], in_=y_acc[2 * pair][:])
+            nc.vector.tensor_copy(out=y[:, 2 * pair + 1, :], in_=y_acc[2 * pair + 1][:])
+            nc.sync.dma_start(out=y_rows[:, 2 * pair : 2 * pair + 2, :], in_=y[:, 2 * pair : 2 * pair + 2, :])
+        y_bf = sb.tile([P, PACK * J], BF16, name="y_bf", align_bytes=64)
+        y_w = sb.tile([P, J], I32, name="y_w", align_bytes=64)
+        y_s = sb.tile([P, J], U8, name="y_s", align_bytes=64)
+        words = out_1[0].rearrange("p c t -> p (c t)").bitcast(I32)
+        weave(nc.vector.tensor_copy, y_bf, y, 0, H)
+        weave(nc.scalar.copy, y_bf, y, H, J)
+        for h in range(2):
+            cols = slice(h * H, (h + 1) * H)
+            nc.vector.quantize_mx(
+                out=y_w[:, cols].bitcast(E4M3), scales=y_s[:, cols], in_=y_bf[:, PACK * h * H : PACK * (h + 1) * H]
+            )
+            nc.sync.dma_start(out=words[:, cols], in_=y_w[:, cols])
+        for q in range(4):
+            queue = nc.scalar if q % 2 else nc.sync
+            queue.dma_start(
+                out=out_2[0, 4 * q : 4 * q + 4, :].bitcast(I32), in_=y_s[32 * q : 32 * q + 4, :].bitcast(I32)
+            )

@@ -51,8 +51,8 @@ def tile_list_product_unit_back_pl_kernel(
         def load_plane(tile, src, t):
             nc.sync.dma_start(out=tile[:], in_=src.rearrange("(p t) c -> p t c", t=PACK)[:, t, :])
 
-        def load_scales(tile, src, first, q):
-            nc.sync.dma_start(
+        def load_scales(tile, src, first, q, queue=nc.sync):
+            queue.dma_start(
                 out=tile[32 * q + first : 32 * q + first + 4, :].bitcast(I32),
                 in_=src[0, 4 * q : 4 * q + 4, :].bitcast(I32),
             )
@@ -65,13 +65,12 @@ def tile_list_product_unit_back_pl_kernel(
             load_plane(g_pl[t], g, t)
         nc.sync.dma_start(out=wd_raw[:], in_=wd_words[0].rearrange("p c t -> p (c t)").bitcast(I32))
         for q in range(4):
-            load_scales(sau_raw, wa_scales, 0, q)
-        nc.sync.dma_start(out=wu_raw[:], in_=wu_words[0].rearrange("p c t -> p (c t)").bitcast(I32))
-        nc.sync.dma_start(out=wa_raw[:].bitcast(I32), in_=wa_words[0].bitcast(I32))
-        load_plane(u_pl[0], u, 0)
+            load_scales(sau_raw, wa_scales, 0, q, nc.gpsimd)
         for q in range(4):
             load_scales(sau_raw, wu_scales, 4, q)
-        for t in range(1, PACK):
+        nc.sync.dma_start(out=wu_raw[:], in_=wu_words[0].rearrange("p c t -> p (c t)").bitcast(I32))
+        nc.sync.dma_start(out=wa_raw[:].bitcast(I32), in_=wa_words[0].bitcast(I32))
+        for t in range(PACK):
             load_plane(u_pl[t], u, t)
         for t in range(PACK):
             load_plane(va_pl[t], va, t)
@@ -82,8 +81,8 @@ def tile_list_product_unit_back_pl_kernel(
                 in_=raw[:].rearrange("p (c i t) -> p c t i", t=PACK, i=4),
             )
 
-        def deal_scales(dealt, raw):
-            nc.vector.tensor_copy(
+        def deal_scales(dealt, raw, engine=nc.vector):
+            engine.tensor_copy(
                 out=dealt[:].rearrange("p (t m) -> p t m", t=PACK),
                 in_=raw[:].rearrange("p (m t) -> p t m", t=PACK),
             )
@@ -98,7 +97,7 @@ def tile_list_product_unit_back_pl_kernel(
             )
         wd_w = sb.tile([P, R], I32, name="wd_w", align_bytes=64)
         wd_s = sb.tile([P, R], U8, name="wd_s", align_bytes=64)
-        deal_scales(wd_s, sd_raw)
+        deal_scales(wd_s, sd_raw, nc.gpsimd)
         deal_words(wd_w, wd_raw)
         g_bf = sb.tile([P, PACK * J], BF16, name="g_bf", tag="after_g", align_bytes=64)
         weave(nc.scalar.copy, g_bf, g_pick, 0, H)
@@ -119,7 +118,10 @@ def tile_list_product_unit_back_pl_kernel(
                 out=acc[:], lhsT=wd_w[:, cols].bitcast(E4M3), lhsT_scale=wd_s[:, cols],
                 rhs=g_w[:].bitcast(E5M2), rhs_scale=g_s[:], start=True, stop=True,
             )
-            if t < PACK - 1:
+            if t == 0:
+                for h in range(2):
+                    nc.scalar.copy(out=dh[t][:, h * H : (h + 1) * H], in_=acc[:, h * H : (h + 1) * H])
+            elif t < PACK - 1:
                 nc.scalar.copy(out=dh[t][:], in_=acc[:])
             else:
                 for h in range(2):
@@ -137,13 +139,17 @@ def tile_list_product_unit_back_pl_kernel(
         wau_s = second[:, 6 * K : 7 * K]
         deal_words(wu_w, wu_raw)
         nc.vector.tensor_copy(
-            out=wa_w[:].rearrange("p (t m b) -> p t m b", t=PACK, b=2),
-            in_=wa_raw[:].rearrange("p (m t b) -> p t m b", t=PACK, b=2),
+            out=wa_w.bitcast(U16).rearrange("p (t m) -> p t m", t=PACK),
+            in_=wa_raw[:].bitcast(U16).rearrange("p (m t) -> p t m", t=PACK),
         )
         deal_scales(wau_s, sau_raw)
 
         da = sb.tile([P, PACK, J], F32, name="da")
-        for t in range(PACK - 1):
+        for h in range(2):
+            nc.vector.tensor_tensor(
+                da[:, 0, h * H : (h + 1) * H], u_pl[0][:].indirect(half_list(h)), dh_half(0, h), MULT
+            )
+        for t in range(1, PACK - 1):
             nc.vector.tensor_tensor(da[:, t, :], u_pl[t][:].indirect(offsets[:]), dh[t][:], MULT)
         for h in range(2):
             nc.vector.tensor_tensor(
@@ -173,8 +179,8 @@ def tile_list_product_unit_back_pl_kernel(
         for t in range(PACK):
             nc.vector.tensor_tensor(du1[:, t, :], va_pl[t][:].indirect(half_list(1)), dh_half(t, 1), MULT)
         du1_bf = sb.tile([P, PACK * H], BF16, name="du1_bf", align_bytes=64)
-        weave(nc.scalar.copy, du1_bf, du1, 0, 96)
-        weave(nc.vector.tensor_copy, du1_bf, du1, 96, H)
+        weave(nc.scalar.copy, du1_bf, du1, 0, 128)
+        weave(nc.vector.tensor_copy, du1_bf, du1, 128, H)
 
         for h, src in enumerate((du0_bf, du1_bf)):
             du_w = sb.tile([P, H], I32, name="du_w%d" % h, align_bytes=64)
@@ -190,16 +196,19 @@ def tile_list_product_unit_back_pl_kernel(
 
         y = sb.tile([P, PACK, J], F32, name="y")
         y_rows = out_0.rearrange("(p t) j -> p t j", t=PACK)
-        for pair in range(2):
-            nc.scalar.copy(out=y[:, 2 * pair, :], in_=y_acc[2 * pair][:])
-            nc.vector.tensor_copy(out=y[:, 2 * pair + 1, :], in_=y_acc[2 * pair + 1][:])
-            nc.sync.dma_start(out=y_rows[:, 2 * pair : 2 * pair + 2, :], in_=y[:, 2 * pair : 2 * pair + 2, :])
+        for t in range(PACK):
+            copy = nc.vector.tensor_copy if t % 2 else nc.scalar.copy
+            copy(out=y[:, t, :], in_=y_acc[t][:])
+            if t < 2:
+                nc.sync.dma_start(out=y_rows[:, t, :], in_=y[:, t, :])
+        nc.sync.dma_start(out=y_rows[:, 2:PACK, :], in_=y[:, 2:PACK, :])
         y_bf = sb.tile([P, PACK * J], BF16, name="y_bf", align_bytes=64)
         y_w = sb.tile([P, J], I32, name="y_w", align_bytes=64)
         y_s = sb.tile([P, J], U8, name="y_s", align_bytes=64)
         words = out_1[0].rearrange("p c t -> p (c t)").bitcast(I32)
         weave(nc.vector.tensor_copy, y_bf, y, 0, H)
-        weave(nc.scalar.copy, y_bf, y, H, J)
+        weave(nc.scalar.copy, y_bf, y, H, J - 64)
+        weave(nc.vector.tensor_copy, y_bf, y, J - 64, J)
         for h in range(2):
             cols = slice(h * H, (h + 1) * H)
             nc.vector.quantize_mx(

@@ -38,7 +38,7 @@ def tile_list_product_unit_back_pl_kernel(
         offsets = sb.tile([P, J // 16], U16, name="offsets")
         g_pl = [sb.tile([P, T], F32, name="g%d" % t) for t in range(PACK)]
         u_pl = [sb.tile([P, T], F32, name="u%d" % t) for t in range(PACK)]
-        va_pl = [sb.tile([P, T], F32, name="va%d" % t) for t in range(PACK)]
+        va_pl = [sb.tile([P, T], F32, name="va%d" % t, tag="va%d" % t, align_bytes=64) for t in range(PACK)]
         wd_raw = sb.tile([P, R], I32, name="wd_raw")
         wu_raw = sb.tile([P, K], I32, name="wu_raw")
         wa_raw = sb.tile([P, 2 * K], U8, name="wa_raw")
@@ -155,18 +155,20 @@ def tile_list_product_unit_back_pl_kernel(
             nc.vector.tensor_tensor(
                 da[:, PACK - 1, h * H : (h + 1) * H], u_pl[PACK - 1][:].indirect(half_list(h)), dh_last[h][:], MULT
             )
-        da_bf = sb.tile([P, PACK * J], BF16, name="da_bf", tag="after_da", align_bytes=64)
+        da_bf = sb.tile([P, PACK * J], BF16, name="da_bf", align_bytes=64)
         weave(nc.scalar.copy, da_bf, da, 0, J)
 
         du0 = sb.tile([P, PACK, H], F32, name="du0")
         for t in range(PACK):
             nc.vector.tensor_tensor(du0[:, t, :], va_pl[t][:].indirect(half_list(0)), dh_half(t, 0), MULT)
-        da_w = sb.tile([P, J], I32, name="da_w", tag="turn", align_bytes=64)
-        da_s = sb.tile([P, J], U8, name="da_s", align_bytes=64)
-        nc.vector.quantize_mx(out=da_w[:].bitcast(E5M2), scales=da_s[:], in_=da_bf[:])
         du0_bf = sb.tile([P, PACK * H], BF16, name="du0_bf", align_bytes=64)
         weave(nc.scalar.copy, du0_bf, du0, 0, H)
 
+        du1 = sb.tile([P, PACK, H], F32, name="du1", tag="turn", align_bytes=64)
+        nc.vector.tensor_tensor(du1[:, 0, :], va_pl[0][:].indirect(half_list(1)), dh_half(0, 1), MULT)
+        da_w = sb.tile([P, J], I32, name="da_w", tag="va0", align_bytes=64)
+        da_s = sb.tile([P, J], U8, name="da_s", align_bytes=64)
+        nc.vector.quantize_mx(out=da_w[:].bitcast(E5M2), scales=da_s[:], in_=da_bf[:])
         y_acc = [ps.tile([P, J], F32, name="y_acc%d" % t) for t in range(PACK)]
         for t in range(PACK):
             cols = slice(t * P, (t + 1) * P)
@@ -175,8 +177,7 @@ def tile_list_product_unit_back_pl_kernel(
                 rhs=da_w[:].bitcast(E5M2), rhs_scale=da_s[:], start=True, stop=False,
             )
 
-        du1 = sb.tile([P, PACK, H], F32, name="du1", tag="after_da", align_bytes=64)
-        for t in range(PACK):
+        for t in range(1, PACK):
             nc.vector.tensor_tensor(du1[:, t, :], va_pl[t][:].indirect(half_list(1)), dh_half(t, 1), MULT)
         du1_bf = sb.tile([P, PACK * H], BF16, name="du1_bf", align_bytes=64)
         weave(nc.scalar.copy, du1_bf, du1, 0, 128)

from contextlib import ExitStack

import concourse.mybir as mybir

K, R, N, T, J = 512, 512, 512, 1024, 512
FLOPS = 3 * 2 * 512 * 512 * J

F32 = mybir.dt.float32
BF16 = mybir.dt.bfloat16
I32 = mybir.dt.int32
U16 = mybir.dt.uint16
U8 = mybir.dt.uint8
E4M3 = mybir.dt.float8_e4m3fn_x4
E5M2 = mybir.dt.float8_e5m2_x4
E2M1 = mybir.dt.float4_e2m1fn_x4
MULT = mybir.AluOpType.mult

P = 128
PACK = 4
H = J // 2


def weave(copy, grouped, planes, lo, hi):
    copy(
        out=grouped[:, PACK * lo : PACK * hi].rearrange("p (c i t) -> p c t i", i=4, t=PACK),
        in_=planes[:, :, lo:hi].rearrange("p t (c i) -> p c t i", i=4),
    )


def tile_list_product_unit_back_pl_kernel(
    tc, g, wd_words, wd_scales, va, u, wa_words, wa_scales, wu_words, wu_scales, offs, out_0, out_1, out_2
):
    nc = tc.nc
    with ExitStack() as ctx:
        sb = ctx.enter_context(tc.tile_pool(name="sb", bufs=1))
        ps = ctx.enter_context(tc.psum_pool(name="ps", bufs=1))

        offsets = sb.tile([P, J // 16], U16, name="offsets")
        g_pl = [sb.tile([P, T], F32, name="g%d" % t) for t in range(PACK)]
        u_pl = [sb.tile([P, T], F32, name="u%d" % t) for t in range(PACK)]
        va_pl = [sb.tile([P, T], F32, name="va%d" % t, tag="va%d" % t, align_bytes=64) for t in range(PACK)]
        wd_raw = sb.tile([P, R], I32, name="wd_raw")
        wu_raw = sb.tile([P, K], I32, name="wu_raw")
        wa_raw = sb.tile([P, 2 * K], U8, name="wa_raw")
        sd_raw = sb.tile([P, R], U8, name="sd_raw")
        sau_raw = sb.tile([P, K], U8, name="sau_raw")

        nc.gpsimd.memset(sd_raw[:].bitcast(I32), 0)
        nc.gpsimd.memset(sau_raw[:].bitcast(I32), 0)

        def load_plane(tile, src, t):
            nc.sync.dma_start(out=tile[:], in_=src.rearrange("(p t) c -> p t c", t=PACK)[:, t, :])

        def load_scales(tile, src, first, q, queue=nc.sync):
            queue.dma_start(
                out=tile[32 * q + first : 32 * q + first + 4, :].bitcast(I32),
                in_=src[0, 4 * q : 4 * q + 4, :].bitcast(I32),
            )

        nc.sync.dma_start(offsets[:], offs)
        load_plane(g_pl[0], g, 0)
        for q in range(4):
            load_scales(sd_raw, wd_scales, 0, q)
        for t in range(1, PACK):
            load_plane(g_pl[t], g, t)
        nc.sync.dma_start(out=wd_raw[:], in_=wd_words[0].rearrange("p c t -> p (c t)").bitcast(I32))
        for q in range(4):
            load_scales(sau_raw, wa_scales, 0, q, nc.gpsimd)
        for q in range(4):
            load_scales(sau_raw, wu_scales, 4, q)
        nc.sync.dma_start(out=wu_raw[:], in_=wu_words[0].rearrange("p c t -> p (c t)").bitcast(I32))
        nc.sync.dma_start(out=wa_raw[:].bitcast(I32), in_=wa_words[0].bitcast(I32))
        for t in range(PACK):
            load_plane(u_pl[t], u, t)
        for t in range(PACK):
            load_plane(va_pl[t], va, t)

        def deal_words(dealt, raw):
            nc.vector.tensor_copy(
                out=dealt[:].rearrange("p (t c i) -> p c t i", t=PACK, i=4),
                in_=raw[:].rearrange("p (c i t) -> p c t i", t=PACK, i=4),
            )

        def deal_scales(dealt, raw, engine=nc.vector):
            engine.tensor_copy(
                out=dealt[:].rearrange("p (t m) -> p t m", t=PACK),
                in_=raw[:].rearrange("p (m t) -> p t m", t=PACK),
            )

        g_pick = sb.tile([P, PACK, J], F32, name="g_pick")
        for t in range(PACK - 1):
            nc.vector.tensor_copy(g_pick[:, t, :], g_pl[t][:].indirect(offsets[:]))
        for h in range(2):
            nc.vector.tensor_copy(
                g_pick[:, PACK - 1, h * H : (h + 1) * H],
                g_pl[PACK - 1][:].indirect(offsets[:, h * H // 16 : (h + 1) * H // 16]),
            )
        wd_w = sb.tile([P, R], I32, name="wd_w", align_bytes=64)
        wd_s = sb.tile([P, R], U8, name="wd_s", align_bytes=64)
        deal_scales(wd_s, sd_raw, nc.gpsimd)
        deal_words(wd_w, wd_raw)
        g_bf = sb.tile([P, PACK * J], BF16, name="g_bf", tag="after_g", align_bytes=64)
        weave(nc.scalar.copy, g_bf, g_pick, 0, H)
        weave(nc.vector.tensor_copy, g_bf, g_pick, H, J)
        g_w = sb.tile([P, J], I32, name="g_w", align_bytes=64)
        g_s = sb.tile([P, J], U8, name="g_s", align_bytes=64)
        nc.vector.quantize_mx(out=g_w[:].bitcast(E5M2), scales=g_s[:], in_=g_bf[:])

        dh = [sb.tile([P, J], F32, name="dh%d" % t) for t in range(PACK - 1)]
        dh_last = [
            sb.tile([P, H], F32, name="dh_last0", tag="turn", align_bytes=64),
            sb.tile([P, H], F32, name="dh_last1"),
        ]
        for t in range(PACK):
            cols = slice(t * P, (t + 1) * P)
            acc = ps.tile([P, J], F32, name="dh_acc%d" % t)
            nc.tensor.matmul_mx(
                out=acc[:], lhsT=wd_w[:, cols].bitcast(E4M3), lhsT_scale=wd_s[:, cols],
                rhs=g_w[:].bitcast(E5M2), rhs_scale=g_s[:], start=True, stop=True,
            )
            if t == 0:
                for h in range(2):
                    nc.scalar.copy(out=dh[t][:, h * H : (h + 1) * H], in_=acc[:, h * H : (h + 1) * H])
            elif t < PACK - 1:
                nc.scalar.copy(out=dh[t][:], in_=acc[:])
            else:
                for h in range(2):
                    nc.scalar.copy(out=dh_last[h][:], in_=acc[:, h * H : (h + 1) * H])

        def dh_half(t, h):
            return dh[t][:, h * H : (h + 1) * H] if t < PACK - 1 else dh_last[h][:]

        def half_list(h):
            return offsets[:, h * H // 16 : (h + 1) * H // 16]

        second = sb.tile([P, 7 * K], U8, name="second", tag="after_g", align_bytes=64)
        wu_w = second[:, 0 : 4 * K].bitcast(I32)
        wa_w = second[:, 4 * K : 6 * K]
        wau_s = second[:, 6 * K : 7 * K]
        deal_words(wu_w, wu_raw)
        nc.vector.tensor_copy(
            out=wa_w.bitcast(U16).rearrange("p (t m) -> p t m", t=PACK),
            in_=wa_raw[:].bitcast(U16).rearrange("p (m t) -> p t m", t=PACK),
        )
        deal_scales(wau_s, sau_raw)

        da = sb.tile([P, PACK, J], F32, name="da")
        for h in range(2):
            nc.vector.tensor_tensor(
                da[:, 0, h * H : (h + 1) * H], u_pl[0][:].indirect(half_list(h)), dh_half(0, h), MULT
            )
        for t in range(1, PACK - 1):
            nc.vector.tensor_tensor(da[:, t, :], u_pl[t][:].indirect(offsets[:]), dh[t][:], MULT)
        for h in range(2):
            nc.vector.tensor_tensor(
                da[:, PACK - 1, h * H : (h + 1) * H], u_pl[PACK - 1][:].indirect(half_list(h)), dh_last[h][:], MULT
            )
        da_bf = sb.tile([P, PACK * J], BF16, name="da_bf", align_bytes=64)
        weave(nc.scalar.copy, da_bf, da, 0, J)

        du0 = sb.tile([P, PACK, H], F32, name="du0")
        for t in range(PACK):
            nc.vector.tensor_tensor(du0[:, t, :], va_pl[t][:].indirect(half_list(0)), dh_half(t, 0), MULT)
        du0_bf = sb.tile([P, PACK * H], BF16, name="du0_bf", align_bytes=64)
        weave(nc.scalar.copy, du0_bf, du0, 0, H)

        du1 = sb.tile([P, PACK, H], F32, name="du1", tag="turn", align_bytes=64)
        nc.vector.tensor_tensor(du1[:, 0, :], va_pl[0][:].indirect(half_list(1)), dh_half(0, 1), MULT)
        da_w = sb.tile([P, J], I32, name="da_w", tag="va0", align_bytes=64)
        da_s = sb.tile([P, J], U8, name="da_s", align_bytes=64)
        nc.vector.quantize_mx(out=da_w[:].bitcast(E5M2), scales=da_s[:], in_=da_bf[:])
        y_acc = [ps.tile([P, J], F32, name="y_acc%d" % t) for t in range(PACK)]
        for t in range(PACK):
            cols = slice(t * P, (t + 1) * P)
            nc.tensor.matmul_mx(
                out=y_acc[t][:], lhsT=wa_w[:, 2 * t * P : 2 * (t + 1) * P].bitcast(E2M1), lhsT_scale=wau_s[:, cols],
                rhs=da_w[:].bitcast(E5M2), rhs_scale=da_s[:], start=True, stop=False,
            )

        for t in range(1, PACK):
            nc.vector.tensor_tensor(du1[:, t, :], va_pl[t][:].indirect(half_list(1)), dh_half(t, 1), MULT)
        du1_bf = sb.tile([P, PACK * H], BF16, name="du1_bf", align_bytes=64)
        weave(nc.scalar.copy, du1_bf, du1, 0, 128)
        weave(nc.vector.tensor_copy, du1_bf, du1, 128, H)

        for h, src in enumerate((du0_bf, du1_bf)):
            du_w = sb.tile([P, H], I32, name="du_w%d" % h, align_bytes=64)
            du_s = sb.tile([P, H], U8, name="du_s%d" % h, align_bytes=64)
            nc.vector.quantize_mx(out=du_w[:].bitcast(E4M3), scales=du_s[:], in_=src[:])
            for t in range(PACK):
                cols = slice(t * P, (t + 1) * P)
                nc.tensor.matmul_mx(
                    out=y_acc[t][:, h * H : (h + 1) * H], lhsT=wu_w[:, cols].bitcast(E4M3),
                    lhsT_scale=wau_s[4:P, cols],
                    rhs=du_w[:].bitcast(E4M3), rhs_scale=du_s[:], start=False, stop=(h == 1),
                )

        y = sb.tile([P, PACK, J], F32, name="y")
        y_rows = out_0.rearrange("(p t) j -> p t j", t=PACK)
        for t in range(PACK):
            copy = nc.vector.tensor_copy if t % 2 else nc.scalar.copy
            copy(out=y[:, t, :], in_=y_acc[t][:])
            if t < 2:
                nc.sync.dma_start(out=y_rows[:, t, :], in_=y[:, t, :])
        nc.sync.dma_start(out=y_rows[:, 2:PACK, :], in_=y[:, 2:PACK, :])
        y_bf = sb.tile([P, PACK * J], BF16, name="y_bf", align_bytes=64)
        y_w = sb.tile([P, J], I32, name="y_w", align_bytes=64)
        y_s = sb.tile([P, J], U8, name="y_s", align_bytes=64)
        words = out_1[0].rearrange("p c t -> p (c t)").bitcast(I32)
        weave(nc.vector.tensor_copy, y_bf, y, 0, H)
        weave(nc.scalar.copy, y_bf, y, H, J - 64)
        weave(nc.vector.tensor_copy, y_bf, y, J - 64, J)
        for h in range(2):
            cols = slice(h * H, (h + 1) * H)
            nc.vector.quantize_mx(
                out=y_w[:, cols].bitcast(E4M3), scales=y_s[:, cols], in_=y_bf[:, PACK * h * H : PACK * (h + 1) * H]
            )
            nc.sync.dma_start(out=words[:, cols], in_=y_w[:, cols])
        for q in range(4):
            queue = nc.scalar if q % 2 else nc.sync
            queue.dma_start(
                out=out_2[0, 4 * q : 4 * q + 4, :].bitcast(I32), in_=y_s[32 * q : 32 * q + 4, :].bitcast(I32)
            )
